import numpy as np
import ml_dtypes


def mxq(x, axis, fmt="e4m3"):
    dtype, down = {"e4m3": (ml_dtypes.float8_e4m3fn, 7), "e5m2": (ml_dtypes.float8_e5m2, 14)}[fmt]
    v = np.moveaxis(np.asarray(x, np.float32).astype(ml_dtypes.bfloat16).astype(np.float64), axis, -1)
    blocks = v.reshape(v.shape[:-1] + (-1, 32))
    amax = np.abs(blocks).max(-1, keepdims=True)
    byte = np.maximum(np.where(amax > 0, np.frexp(amax)[1] - 1 + 127, 0) - down, 1)
    scale = np.exp2(byte - 127.0)
    codes = (blocks / scale).astype(np.float32).astype(dtype).astype(np.float64)
    return np.moveaxis((codes * scale).reshape(v.shape), -1, axis)


WIDE = False


def mx_kscale(k):
    if not WIDE:
        return np.ones(k)
    levels = np.array([10, -10, 5, -5, 0])
    if k % 512:
        return np.exp2(np.random.permutation(np.resize(levels, k // 32))).repeat(32)
    a = np.empty((k // 512, 16))
    for p in range(k // 512):
        a[p, :8] = np.random.permutation(np.resize(levels, 8))
        for g in range(8):
            far = levels[np.abs(levels - a[p, g]) >= 10]
            a[p, g + 8] = far[np.random.randint(len(far))]
    return np.exp2(a.ravel()).repeat(32)


def f64(x):
    return np.asarray(x).astype(np.float64)


def striped(idx):
    return np.tile(idx.reshape(-1, 16).T, (8, 1)).astype(np.uint16)


def unstriped(offs):
    return offs[:16].T.reshape(-1).astype(np.int64)


E2M1 = np.array([0.0, 0.5, 1.0, 1.5, 2.0, 3.0, 4.0, 6.0, -0.0, -0.5, -1.0, -1.5, -2.0, -3.0, -4.0, -6.0])


def pack_weight(w, fmt):
    k, n = w.shape
    w = f64(np.asarray(w, np.float32).astype(ml_dtypes.bfloat16)).reshape(k // 32, 32, n)
    amax = np.abs(w).max(1)
    if fmt == "e4m3":
        byte = np.frexp(amax)[1] - 1 + 127 - 7
    else:
        mant, ex = np.frexp(amax / 6.0)
        byte = np.where(mant > 0.5, ex, ex - 1) + 127
    byte = np.clip(np.where(amax > 0, byte, 1), 1, 254)
    scaled = (w * np.exp2(127.0 - byte)[:, None, :]).reshape(k, n).astype(np.float32)
    by_word = np.ascontiguousarray(scaled.reshape(k // 512, 128, 4, n).transpose(0, 1, 3, 2))
    if fmt == "e4m3":
        words = by_word.astype(ml_dtypes.float8_e4m3fn).view(np.uint8)
    else:
        c = by_word.astype(ml_dtypes.float4_e2m1fn).view(np.uint8) & 0xF
        words = (c[..., 0::2] | (c[..., 1::2] << 4)).reshape(k // 512, 128, 2 * n)
    return np.ascontiguousarray(words), np.ascontiguousarray(byte.astype(np.uint8).reshape(k // 512, 16, n))


def unpack_weight(words, scales, fmt):
    g, _, n = scales.shape
    words = np.ascontiguousarray(words).reshape(g, 128, n, -1)
    if fmt == "e4m3":
        vals = words.view(ml_dtypes.float8_e4m3fn).astype(np.float64)
    else:
        nib = np.empty((g, 128, n, 4), np.uint8)
        nib[..., 0::2] = words & 0xF
        nib[..., 1::2] = words >> 4
        vals = E2M1[nib]
    vals = vals * np.repeat(np.exp2(scales.astype(np.float64) - 127.0), 8, axis=1)[..., None]
    return vals.transpose(0, 1, 3, 2).reshape(g * 512, n)


def pack_table(v):
    words, scales = pack_weight(v, "e4m3")
    return np.concatenate([words.reshape(words.shape[0], -1), scales.reshape(scales.shape[0], -1)], axis=1)


def unpack_table(tab):
    g, t = tab.shape[0], tab.shape[1] // 528
    return unpack_weight(tab[:, :512 * t].reshape(g, 128, t, 4), tab[:, 512 * t:].reshape(g, 16, t), "e4m3")


G, K, M, T, S = 5, 512, 512, 4096, 512


def setup_inputs():
    n = np.random.standard_normal
    s = mx_kscale(K)[:, None]
    return {
        "tab": pack_table(n((K, T)) * s),
        "w": (n((K, M)) / np.sqrt(K) / s).astype(np.float32),
        "offs": striped(np.concatenate([np.random.permutation(T)[:S] for _ in range(G)])),
    }


def reference(tab, w, offs):
    tab_ = unpack_table(tab)[:, unstriped(offs).reshape(G, S)].sum(1)
    w_ = mxq(f64(w), 0, "e4m3")
    y = w_.T @ tab_
    return y

@@ -1,0 +1,134 @@
+from contextlib import ExitStack
+
+import concourse.mybir as mybir
+
+G, K, M, T, S = 5, 512, 512, 4096, 512
+FLOPS = 2 * G * K * M * S
+
+F32 = mybir.dt.float32
+BF16 = mybir.dt.bfloat16
+I32 = mybir.dt.int32
+U32 = mybir.dt.uint32
+U16 = mybir.dt.uint16
+U8 = mybir.dt.uint8
+FP8X4 = mybir.dt.float8_e4m3fn_x4
+
+P = 128
+PACK = 4
+LIST_ROWS = 16
+SCALE_ROWS = 16
+QUADRANT = 32
+FIRST_SCALE_ROW = P - SCALE_ROWS
+M_TILE = 128
+HALF = S // 2
+W_HALF = M // 2
+SCALE_CUTS = ((0, 2), (2, 5))
+
+
+def tile_list_tabbag_none_kernel(tc, tab, w, offs, out):
+    nc = tc.nc
+    with ExitStack() as ctx:
+        keep = ctx.enter_context(tc.tile_pool(name="keep", bufs=1))
+        psum = ctx.enter_context(tc.psum_pool(name="psum", bufs=1))
+
+        offsets = keep.tile([P, G * S // LIST_ROWS], U16, name="offsets")
+        tab_scales = keep.tile([P, T], U8, name="tab_scales", align_bytes=64)
+        tab_words = keep.tile([P, T], U32, name="tab_words", align_bytes=64)
+
+        scale_rows = tab[0, K * T : (K + SCALE_ROWS) * T].rearrange("(q t) -> q t", q=SCALE_ROWS)
+        nc.sync.dma_start(out=tab_scales[FIRST_SCALE_ROW:P, :].bitcast(I32), in_=scale_rows.bitcast(I32))
+        nc.sync.dma_start(offsets[:], offs)
+        nc.vector.memset(tab_scales[0:FIRST_SCALE_ROW, :].bitcast(I32), 0)
+
+        w_by_row = w.rearrange("(p i) n -> p i n", i=PACK)
+        w_raw = [keep.tile([P, PACK, W_HALF], F32, name="w_raw%d" % h) for h in range(2)]
+        word_rows = tab[0, 0 : K * T].rearrange("(p b) -> p b", p=P)
+        nc.sync.dma_start(out=w_raw[0][:], in_=w_by_row[:, :, 0:W_HALF])
+        nc.sync.dma_start(out=w_raw[1][:], in_=w_by_row[:, :, W_HALF:M])
+        nc.sync.dma_start(out=tab_words[:].bitcast(I32), in_=word_rows.bitcast(I32))
+
+        def list_slice(g0, g1):
+            return offsets[:, g0 * S // LIST_ROWS : g1 * S // LIST_ROWS]
+
+        planes = {}
+        picked = []
+        for g0, g1 in SCALE_CUTS:
+            plane = keep.tile([P, (g1 - g0) * S], U8, name="plane%d" % g0, align_bytes=64)
+            nc.gpsimd.memset(plane[:].bitcast(I32), 0)
+            for g in range(g0, g1):
+                planes[g] = plane[:, (g - g0) * S : (g - g0 + 1) * S]
+            picked.append(plane)
+
+        w_grouped = []
+        for h in range(2):
+            grouped = keep.tile([P, W_HALF, PACK], BF16, name="w_grouped%d" % h, align_bytes=64)
+            nc.scalar.copy(out=grouped[:], in_=w_raw[h][:].rearrange("p i n -> p n i"))
+            w_grouped.append(grouped)
+
+        for (g0, g1), plane, queue in zip(SCALE_CUTS, picked, (nc.sync, nc.sync)):
+            rows = keep.tile([P, (g1 - g0) * S], U8, name="picked_scales%d" % g0, align_bytes=64)
+            nc.vector.tensor_copy(rows[:], tab_scales[:].indirect(list_slice(g0, g1)))
+            for q in range(P // QUADRANT):
+                src = FIRST_SCALE_ROW + PACK * q
+                queue.dma_start(
+                    out=plane[QUADRANT * q : QUADRANT * q + PACK, :].bitcast(I32),
+                    in_=rows[src : src + PACK, :].bitcast(I32),
+                )
+
+        w_codes = [keep.tile([P, W_HALF], U32, name="w_codes%d" % h, align_bytes=64) for h in range(2)]
+        w_scales = [keep.tile([P, W_HALF], U8, name="w_scales%d" % h, align_bytes=64) for h in range(2)]
+
+        def quantize_w(h):
+            nc.vector.quantize_mx(
+                out=w_codes[h][:].bitcast(FP8X4),
+                scales=w_scales[h][:],
+                in_=w_grouped[h][:].rearrange("p n i -> p (n i)"),
+            )
+
+        banks = {}
+        for m in range(M // M_TILE):
+            for u in range(2):
+                banks[m, u] = psum.tile([M_TILE, S], F32, name="bank%d_%d" % (m, u))
+
+        words = [keep.tile([P, S], U32, name="picked_words%d" % g, align_bytes=64) for g in range(G)]
+
+        def gather_words(g):
+            nc.vector.tensor_copy(words[g][:], tab_words[:].indirect(list_slice(g, g + 1)))
+
+        def multiply(g, h):
+            for m in (2 * h, 2 * h + 1):
+                c0 = m * M_TILE - h * W_HALF
+                for u in range(2):
+                    cols = slice(u * HALF, (u + 1) * HALF)
+                    nc.tensor.matmul_mx(
+                        out=banks[m, u][:, 0:HALF],
+                        lhsT=w_codes[h][:, c0 : c0 + M_TILE].bitcast(FP8X4),
+                        lhsT_scale=w_scales[h][:, c0 : c0 + M_TILE],
+                        rhs=words[g][:, cols].bitcast(FP8X4),
+                        rhs_scale=planes[g][:, cols],
+                        start=(g == 0),
+                        stop=(g == G - 1),
+                    )
+
+        quantize_w(0)
+        quantize_w(1)
+        for i in range(4):
+            nc.tensor.matmul_mx(
+                out=banks[i, 0][:, HALF:S],
+                lhsT=w_codes[0][:, 0:M_TILE].bitcast(FP8X4),
+                lhsT_scale=w_scales[0][:, 0:M_TILE],
+                rhs=w_codes[1][:].bitcast(FP8X4),
+                rhs_scale=w_scales[1][:],
+                start=True,
+                stop=True,
+            )
+        for g in range(G):
+            gather_words(g)
+            multiply(g, 0)
+            multiply(g, 1)
+
+        for m in range(M // M_TILE):
+            result = keep.tile([M_TILE, S], F32, name="result%d" % m)
+            nc.scalar.copy(out=result[:, 0:HALF], in_=banks[m, 0][:, 0:HALF])
+            nc.vector.tensor_copy(out=result[:, HALF:S], in_=banks[m, 1][:, 0:HALF])
+            nc.sync.dma_start(out=out[m * M_TILE : (m + 1) * M_TILE, :], in_=result[:])

@@ -22,7 +22,7 @@ FIRST_SCALE_ROW = P - SCALE_ROWS
 M_TILE = 128
 HALF = S // 2
 W_HALF = M // 2
-SCALE_CUTS = ((0, 2), (2, 5))
+SCALE_CUTS = ((0, 4), (4, 5))
 
 
 def tile_list_tabbag_none_kernel(tc, tab, w, offs, out):
@@ -41,10 +41,9 @@ def tile_list_tabbag_none_kernel(tc, tab, w, offs, out):
         nc.vector.memset(tab_scales[0:FIRST_SCALE_ROW, :].bitcast(I32), 0)
 
         w_by_row = w.rearrange("(p i) n -> p i n", i=PACK)
-        w_raw = [keep.tile([P, PACK, W_HALF], F32, name="w_raw%d" % h) for h in range(2)]
+        w_raw = keep.tile([P, PACK, M], F32, name="w_raw")
         word_rows = tab[0, 0 : K * T].rearrange("(p b) -> p b", p=P)
-        nc.sync.dma_start(out=w_raw[0][:], in_=w_by_row[:, :, 0:W_HALF])
-        nc.sync.dma_start(out=w_raw[1][:], in_=w_by_row[:, :, W_HALF:M])
+        nc.sync.dma_start(out=w_raw[:], in_=w_by_row)
         nc.sync.dma_start(out=tab_words[:].bitcast(I32), in_=word_rows.bitcast(I32))
 
         def list_slice(g0, g1):
@@ -62,7 +61,7 @@ def tile_list_tabbag_none_kernel(tc, tab, w, offs, out):
         w_grouped = []
         for h in range(2):
             grouped = keep.tile([P, W_HALF, PACK], BF16, name="w_grouped%d" % h, align_bytes=64)
-            nc.scalar.copy(out=grouped[:], in_=w_raw[h][:].rearrange("p i n -> p n i"))
+            nc.scalar.copy(out=grouped[:], in_=w_raw[:, :, h * W_HALF : (h + 1) * W_HALF].rearrange("p i n -> p n i"))
             w_grouped.append(grouped)
 
         for (g0, g1), plane, queue in zip(SCALE_CUTS, picked, (nc.sync, nc.sync)):
@@ -114,11 +113,11 @@ def tile_list_tabbag_none_kernel(tc, tab, w, offs, out):
         quantize_w(1)
         for i in range(4):
             nc.tensor.matmul_mx(
-                out=banks[i, 0][:, HALF:S],
+                out=banks[2 + i // 2, i % 2][:, HALF:S],
                 lhsT=w_codes[0][:, 0:M_TILE].bitcast(FP8X4),
                 lhsT_scale=w_scales[0][:, 0:M_TILE],
-                rhs=w_codes[1][:].bitcast(FP8X4),
-                rhs_scale=w_scales[1][:],
+                rhs=w_codes[0][:].bitcast(FP8X4),
+                rhs_scale=w_scales[0][:],
                 start=True,
                 stop=True,
             )

@@ -22,7 +22,8 @@ FIRST_SCALE_ROW = P - SCALE_ROWS
 M_TILE = 128
 HALF = S // 2
 W_HALF = M // 2
-SCALE_CUTS = ((0, 4), (4, 5))
+SCALE_CUTS = ((0, 1), (1, 5))
+WORD_CUTS = ((0, 2), (2, 4), (4, 6), (6, 9), (8, 10))
 
 
 def tile_list_tabbag_none_kernel(tc, tab, w, offs, out):
@@ -89,25 +90,31 @@ def tile_list_tabbag_none_kernel(tc, tab, w, offs, out):
             for u in range(2):
                 banks[m, u] = psum.tile([M_TILE, S], F32, name="bank%d_%d" % (m, u))
 
-        words = [keep.tile([P, S], U32, name="picked_words%d" % g, align_bytes=64) for g in range(G)]
+        words = {}
 
-        def gather_words(g):
-            nc.vector.tensor_copy(words[g][:], tab_words[:].indirect(list_slice(g, g + 1)))
+        def gather_words(v0, v1):
+            picked_words = keep.tile([P, (v1 - v0) * HALF], U32, name="picked_words%d" % v0, align_bytes=64)
+            span = offsets[:, v0 * HALF // LIST_ROWS : v1 * HALF // LIST_ROWS]
+            nc.vector.tensor_copy(picked_words[:], tab_words[:].indirect(span))
+            for v in range(v0, v1):
+                words.setdefault(v, picked_words[:, (v - v0) * HALF : (v - v0 + 1) * HALF])
 
-        def multiply(g, h):
-            for m in (2 * h, 2 * h + 1):
-                c0 = m * M_TILE - h * W_HALF
-                for u in range(2):
-                    cols = slice(u * HALF, (u + 1) * HALF)
-                    nc.tensor.matmul_mx(
-                        out=banks[m, u][:, 0:HALF],
-                        lhsT=w_codes[h][:, c0 : c0 + M_TILE].bitcast(FP8X4),
-                        lhsT_scale=w_scales[h][:, c0 : c0 + M_TILE],
-                        rhs=words[g][:, cols].bitcast(FP8X4),
-                        rhs_scale=planes[g][:, cols],
-                        start=(g == 0),
-                        stop=(g == G - 1),
-                    )
+        def multiply(m, g, u):
+            h, c0 = divmod(m * M_TILE, W_HALF)
+            nc.tensor.matmul_mx(
+                out=banks[m, u][:, 0:HALF],
+                lhsT=w_codes[h][:, c0 : c0 + M_TILE].bitcast(FP8X4),
+                lhsT_scale=w_scales[h][:, c0 : c0 + M_TILE],
+                rhs=words[2 * g + u].bitcast(FP8X4),
+                rhs_scale=planes[g][:, u * HALF : (u + 1) * HALF],
+                start=(g == 0),
+                stop=(g == G - 1),
+            )
+
+        def store(m, u, copy):
+            result = keep.tile([M_TILE, HALF], F32, name="result%d_%d" % (m, u))
+            copy(out=result[:], in_=banks[m, u][:, 0:HALF])
+            nc.sync.dma_start(out=out[m * M_TILE : (m + 1) * M_TILE, u * HALF : (u + 1) * HALF], in_=result[:])
 
         quantize_w(0)
         quantize_w(1)
@@ -121,13 +128,15 @@ def tile_list_tabbag_none_kernel(tc, tab, w, offs, out):
                 start=True,
                 stop=True,
             )
-        for g in range(G):
-            gather_words(g)
-            multiply(g, 0)
-            multiply(g, 1)
-
-        for m in range(M // M_TILE):
-            result = keep.tile([M_TILE, S], F32, name="result%d" % m)
-            nc.scalar.copy(out=result[:, 0:HALF], in_=banks[m, 0][:, 0:HALF])
-            nc.vector.tensor_copy(out=result[:, HALF:S], in_=banks[m, 1][:, 0:HALF])
-            nc.sync.dma_start(out=out[m * M_TILE : (m + 1) * M_TILE, :], in_=result[:])
+        m_tiles = range(M // M_TILE)
+        for g in range(G - 2):
+            gather_words(*WORD_CUTS[g])
+            for m in m_tiles:
+                multiply(m, g, 0)
+                multiply(m, g, 1)
+        for u in range(2):
+            gather_words(*WORD_CUTS[G - 2 + u])
+            for m in m_tiles:
+                multiply(m, G - 2, u)
+                multiply(m, G - 1, u)
+                store(m, u, nc.vector.tensor_copy if (u == 1 and m % 2 == 1) else nc.scalar.copy)

from contextlib import ExitStack

import concourse.mybir as mybir

G, K, M, T, S = 5, 512, 512, 4096, 512
FLOPS = 2 * G * K * M * S

F32 = mybir.dt.float32
BF16 = mybir.dt.bfloat16
I32 = mybir.dt.int32
U32 = mybir.dt.uint32
U16 = mybir.dt.uint16
U8 = mybir.dt.uint8
FP8X4 = mybir.dt.float8_e4m3fn_x4

P = 128
PACK = 4
LIST_ROWS = 16
SCALE_ROWS = 16
QUADRANT = 32
FIRST_SCALE_ROW = P - SCALE_ROWS
M_TILE = 128
HALF = S // 2
W_HALF = M // 2
SCALE_CUTS = ((0, 1), (1, 5))
WORD_CUTS = ((0, 2), (2, 4), (4, 6), (6, 9), (8, 10))


def tile_list_tabbag_none_kernel(tc, tab, w, offs, out):
    nc = tc.nc
    with ExitStack() as ctx:
        keep = ctx.enter_context(tc.tile_pool(name="keep", bufs=1))
        psum = ctx.enter_context(tc.psum_pool(name="psum", bufs=1))

        offsets = keep.tile([P, G * S // LIST_ROWS], U16, name="offsets")
        tab_scales = keep.tile([P, T], U8, name="tab_scales", align_bytes=64)
        tab_words = keep.tile([P, T], U32, name="tab_words", align_bytes=64)

        scale_rows = tab[0, K * T : (K + SCALE_ROWS) * T].rearrange("(q t) -> q t", q=SCALE_ROWS)
        nc.sync.dma_start(out=tab_scales[FIRST_SCALE_ROW:P, :].bitcast(I32), in_=scale_rows.bitcast(I32))
        nc.sync.dma_start(offsets[:], offs)
        nc.vector.memset(tab_scales[0:FIRST_SCALE_ROW, :].bitcast(I32), 0)

        w_by_row = w.rearrange("(p i) n -> p i n", i=PACK)
        w_raw = keep.tile([P, PACK, M], F32, name="w_raw")
        word_rows = tab[0, 0 : K * T].rearrange("(p b) -> p b", p=P)
        nc.sync.dma_start(out=w_raw[:], in_=w_by_row)
        nc.sync.dma_start(out=tab_words[:].bitcast(I32), in_=word_rows.bitcast(I32))

        def list_slice(g0, g1):
            return offsets[:, g0 * S // LIST_ROWS : g1 * S // LIST_ROWS]

        planes = {}
        picked = []
        for g0, g1 in SCALE_CUTS:
            plane = keep.tile([P, (g1 - g0) * S], U8, name="plane%d" % g0, align_bytes=64)
            nc.gpsimd.memset(plane[:].bitcast(I32), 0)
            for g in range(g0, g1):
                planes[g] = plane[:, (g - g0) * S : (g - g0 + 1) * S]
            picked.append(plane)

        w_grouped = []
        for h in range(2):
            grouped = keep.tile([P, W_HALF, PACK], BF16, name="w_grouped%d" % h, align_bytes=64)
            nc.scalar.copy(out=grouped[:], in_=w_raw[:, :, h * W_HALF : (h + 1) * W_HALF].rearrange("p i n -> p n i"))
            w_grouped.append(grouped)

        for (g0, g1), plane, queue in zip(SCALE_CUTS, picked, (nc.sync, nc.sync)):
            rows = keep.tile([P, (g1 - g0) * S], U8, name="picked_scales%d" % g0, align_bytes=64)
            nc.vector.tensor_copy(rows[:], tab_scales[:].indirect(list_slice(g0, g1)))
            for q in range(P // QUADRANT):
                src = FIRST_SCALE_ROW + PACK * q
                queue.dma_start(
                    out=plane[QUADRANT * q : QUADRANT * q + PACK, :].bitcast(I32),
                    in_=rows[src : src + PACK, :].bitcast(I32),
                )

        w_codes = [keep.tile([P, W_HALF], U32, name="w_codes%d" % h, align_bytes=64) for h in range(2)]
        w_scales = [keep.tile([P, W_HALF], U8, name="w_scales%d" % h, align_bytes=64) for h in range(2)]

        def quantize_w(h):
            nc.vector.quantize_mx(
                out=w_codes[h][:].bitcast(FP8X4),
                scales=w_scales[h][:],
                in_=w_grouped[h][:].rearrange("p n i -> p (n i)"),
            )

        banks = {}
        for m in range(M // M_TILE):
            for u in range(2):
                banks[m, u] = psum.tile([M_TILE, S], F32, name="bank%d_%d" % (m, u))

        words = {}

        def gather_words(v0, v1):
            picked_words = keep.tile([P, (v1 - v0) * HALF], U32, name="picked_words%d" % v0, align_bytes=64)
            span = offsets[:, v0 * HALF // LIST_ROWS : v1 * HALF // LIST_ROWS]
            nc.vector.tensor_copy(picked_words[:], tab_words[:].indirect(span))
            for v in range(v0, v1):
                words.setdefault(v, picked_words[:, (v - v0) * HALF : (v - v0 + 1) * HALF])

        def multiply(m, g, u):
            h, c0 = divmod(m * M_TILE, W_HALF)
            nc.tensor.matmul_mx(
                out=banks[m, u][:, 0:HALF],
                lhsT=w_codes[h][:, c0 : c0 + M_TILE].bitcast(FP8X4),
                lhsT_scale=w_scales[h][:, c0 : c0 + M_TILE],
                rhs=words[2 * g + u].bitcast(FP8X4),
                rhs_scale=planes[g][:, u * HALF : (u + 1) * HALF],
                start=(g == 0),
                stop=(g == G - 1),
            )

        def store(m, u, copy):
            result = keep.tile([M_TILE, HALF], F32, name="result%d_%d" % (m, u))
            copy(out=result[:], in_=banks[m, u][:, 0:HALF])
            nc.sync.dma_start(out=out[m * M_TILE : (m + 1) * M_TILE, u * HALF : (u + 1) * HALF], in_=result[:])

        quantize_w(0)
        quantize_w(1)
        for i in range(4):
            nc.tensor.matmul_mx(
                out=banks[2 + i // 2, i % 2][:, HALF:S],
                lhsT=w_codes[0][:, 0:M_TILE].bitcast(FP8X4),
                lhsT_scale=w_scales[0][:, 0:M_TILE],
                rhs=w_codes[0][:].bitcast(FP8X4),
                rhs_scale=w_scales[0][:],
                start=True,
                stop=True,
            )
        m_tiles = range(M // M_TILE)
        for g in range(G - 2):
            gather_words(*WORD_CUTS[g])
            for m in m_tiles:
                multiply(m, g, 0)
                multiply(m, g, 1)
        for u in range(2):
            gather_words(*WORD_CUTS[G - 2 + u])
            for m in m_tiles:
                multiply(m, G - 2, u)
                multiply(m, G - 1, u)
                store(m, u, nc.vector.tensor_copy if (u == 1 and m % 2 == 1) else nc.scalar.copy)
